import numpy as np
import ml_dtypes


def mxq(x, axis, fmt="e4m3"):
    dtype, down = {"e4m3": (ml_dtypes.float8_e4m3fn, 7), "e5m2": (ml_dtypes.float8_e5m2, 14)}[fmt]
    v = np.moveaxis(np.asarray(x, np.float32).astype(ml_dtypes.bfloat16).astype(np.float64), axis, -1)
    blocks = v.reshape(v.shape[:-1] + (-1, 32))
    amax = np.abs(blocks).max(-1, keepdims=True)
    byte = np.maximum(np.where(amax > 0, np.frexp(amax)[1] - 1 + 127, 0) - down, 1)
    scale = np.exp2(byte - 127.0)
    codes = (blocks / scale).astype(np.float32).astype(dtype).astype(np.float64)
    return np.moveaxis((codes * scale).reshape(v.shape), -1, axis)


WIDE = False


def mx_kscale(k):
    if not WIDE:
        return np.ones(k)
    levels = np.array([10, -10, 5, -5, 0])
    if k % 512:
        return np.exp2(np.random.permutation(np.resize(levels, k // 32))).repeat(32)
    a = np.empty((k // 512, 16))
    for p in range(k // 512):
        a[p, :8] = np.random.permutation(np.resize(levels, 8))
        for g in range(8):
            far = levels[np.abs(levels - a[p, g]) >= 10]
            a[p, g + 8] = far[np.random.randint(len(far))]
    return np.exp2(a.ravel()).repeat(32)


def f64(x):
    return np.asarray(x).astype(np.float64)


def striped(idx):
    return np.tile(idx.reshape(-1, 16).T, (8, 1)).astype(np.uint16)


def unstriped(offs):
    return offs[:16].T.reshape(-1).astype(np.int64)


def striped8(idx):
    return np.concatenate([x.reshape(-1, 16).T for x in idx]).astype(np.uint16)


def runs(offs, k):
    lists = np.stack([offs[16 * r : 16 * r + 16].T.reshape(-1) for r in range(8)]).astype(np.int64)
    return lists[np.arange(k) % 512 // 64]


def pack_weight(w):
    k, n = w.shape
    w = f64(np.asarray(w, np.float32).astype(ml_dtypes.bfloat16)).reshape(k // 32, 32, n)
    amax = np.abs(w).max(1)
    byte = np.clip(np.where(amax > 0, np.frexp(amax)[1] - 1 + 127 - 7, 1), 1, 254)
    scaled = (w * np.exp2(127.0 - byte)[:, None, :]).reshape(k, n).astype(np.float32)
    words = np.ascontiguousarray(scaled.reshape(k // 512, 128, 4, n).transpose(0, 1, 3, 2)).astype(ml_dtypes.float8_e4m3fn).view(np.uint8)
    return words, np.ascontiguousarray(byte.astype(np.uint8).reshape(k // 512, 16, n))


def unpack_weight(words, scales):
    g, p, n, _ = words.shape
    vals = np.ascontiguousarray(words).view(ml_dtypes.float8_e4m3fn).astype(np.float64) * np.repeat(np.exp2(scales.astype(np.float64) - 127.0), 8, axis=1)[..., None]
    return vals.transpose(0, 1, 3, 2).reshape(g * 512, n)

def planes(y):
    n, m = y.shape
    v = y.astype(np.float32).astype(ml_dtypes.bfloat16).astype(np.float64).reshape(n // 32, 32, m)
    top = np.abs(v).max(1)
    byte = np.clip(np.where(top > 0, np.frexp(top)[1] - 1 + 127 - 7, 1), 1, 254)
    codes = (v * np.exp2(127.0 - byte)[:, None, :]).reshape(n, m).astype(np.float32).astype(ml_dtypes.float8_e4m3fn).view(np.uint8)
    words = codes.reshape(n // 512, 128, 4, m).transpose(0, 1, 3, 2)
    return np.ascontiguousarray(words), np.ascontiguousarray(byte.astype(np.uint8).reshape(n // 512, 16, m))


K, T, S, H, W = 512, 2048, 512, 512, 256


def setup_inputs():
    n = np.random.standard_normal
    s = mx_kscale(K)[:, None]
    u = mx_kscale(S)
    packed_xT = pack_weight(n((K, T)) * s)
    packed_w1 = pack_weight(n((K, H)) / np.sqrt(K) / s)
    perm = np.stack([np.random.permutation(S) for _ in range(8)])
    return {
        "x_words": packed_xT[0],
        "x_scales": packed_xT[1],
        "w1_words": packed_w1[0],
        "w1_scales": packed_w1[1],
        "ga": (np.random.uniform(0.5, 1.5, (H, 1)) * u[:, None]).astype(np.float32),
        "gb": (np.random.uniform(0.5, 1.5, (H, 1)) / u[:, None]).astype(np.float32),
        "offs": striped(np.random.permutation(T)[:S]),
        "n1": striped8(perm[:, :W]),
        "n2": striped8(perm[:, W:]),
        "n3": striped(np.random.permutation(S)),
        "n4": striped(np.random.permutation(S)),
        "n5": striped(np.random.permutation(S)),
        "n6": striped8(np.stack([np.random.permutation(S) for _ in range(8)])),
    }


def reference(x_words, x_scales, w1_words, w1_scales, ga, gb, offs, n1, n2, n3, n4, n5, n6):
    xq = unpack_weight(x_words, x_scales)[:, unstriped(offs)]
    y = unpack_weight(w1_words, w1_scales).T @ xq
    pa = y[np.arange(H)[:, None], runs(n1, H)]
    pb = y[np.arange(H)[:, None], runs(n2, H)]
    ra = np.maximum(pa, pb)
    ds = y.copy()
    ds[np.arange(H)[:, None], runs(n1, H)] = ra
    z = f64(ga) * ds
    ex = np.exp(0.5 * y)
    z2 = f64(gb) * (np.log((ex + ex[:, unstriped(n3)]) / (ex[:, unstriped(n4)] + ex[:, unstriped(n5)])))
    s = 0.0625 * ((mxq(z, 0, "e4m3").T @ mxq(z2, 0, "e4m3")))
    pa2 = s[np.arange(S)[:, None], runs(n6, S)]
    out_0 = (2.0 * (s * pa2)) / ((s) ** 2 + (pa2) ** 2 + 0.5)
    return (out_0,) + planes(out_0)

@@ -1,0 +1,256 @@
+from contextlib import ExitStack
+
+import concourse.mybir as mybir
+
+F32 = mybir.dt.float32
+BF16 = mybir.dt.bfloat16
+I32 = mybir.dt.int32
+U32 = mybir.dt.uint32
+U16 = mybir.dt.uint16
+U8 = mybir.dt.uint8
+FP8X4 = mybir.dt.float8_e4m3fn_x4
+ACT = mybir.ActivationFunctionType
+ALU = mybir.AluOpType
+
+P = 128
+PACK = 4
+T, S, W = 2048, 512, 256
+FLOPS = 2 * 2 * 512 * 512 * 512
+
+Z2_PIECES = ((0, 256), (256, 384), (384, 512))
+OUT_PIECES = ((0, 256), (256, 512))
+
+
+def tile_picked_selffilloddsharm_none_po_kernel(
+    tc, x_words, x_scales, w1_words, w1_scales, ga, gb, offs, n1, n2, n3, n4, n5, n6, out_0, out_1, out_2
+):
+    nc = tc.nc
+    with ExitStack() as ctx:
+        pool = ctx.enter_context(tc.tile_pool(name="held", bufs=1))
+        psum = ctx.enter_context(tc.psum_pool(name="psum", bufs=1))
+
+        def sb(name, shape, dtype):
+            return pool.tile(shape, dtype, name=name, align_bytes=64)
+
+        def load_list(name, src, entries):
+            tile = sb(name, [P, entries // 16], U16)
+            nc.sync.dma_start(tile[:], src)
+            return tile
+
+        def scale_rows(tile, q):
+            return tile[32 * q : 32 * q + 4, :].bitcast(I32)
+
+        def load_scales(queue, tile, src, q):
+            rows = src[0, 4 * q : 4 * q + 4, :].bitcast(I32)
+            queue.dma_start(out=tile[32 * q : 32 * q + 32, :].bitcast(I32), in_=rows.partition_broadcast(8))
+
+        xs = sb("xs", [P, T], U8)
+        ws = sb("ws", [P, S], U8)
+        xw = sb("xw", [P, T], U32)
+        ww = sb("ww", [P, S], U32)
+        l_offs = load_list("l_offs", offs, S)
+        load_scales(nc.scalar, xs, x_scales, 2)
+        load_scales(nc.sync, xs, x_scales, 0)
+        load_scales(nc.scalar, xs, x_scales, 3)
+        load_scales(nc.sync, xs, x_scales, 1)
+        load_scales(nc.scalar, ws, w1_scales, 0)
+        nc.sync.dma_start(out=xw[:].bitcast(I32), in_=x_words[0].rearrange("p n t -> p (n t)").bitcast(I32))
+        load_scales(nc.scalar, ws, w1_scales, 1)
+        nc.sync.dma_start(out=ww[:].bitcast(I32), in_=w1_words[0].rearrange("p n t -> p (n t)").bitcast(I32))
+        load_scales(nc.scalar, ws, w1_scales, 2)
+        load_scales(nc.scalar, ws, w1_scales, 3)
+        l_n2 = load_list("l_n2", n2, W)
+        l_n1 = load_list("l_n1", n1, W)
+        ga_t = sb("ga_t", [P, PACK], F32)
+        nc.sync.dma_start(out=ga_t[:], in_=ga.rearrange("(p t) o -> p (t o)", t=PACK))
+        l_n3 = load_list("l_n3", n3, S)
+        l_n4 = load_list("l_n4", n4, S)
+        l_n5 = load_list("l_n5", n5, S)
+        gb_t = sb("gb_t", [P, PACK], F32)
+        nc.sync.dma_start(out=gb_t[:], in_=gb.rearrange("(p t) o -> p (t o)", t=PACK))
+        l_n6 = load_list("l_n6", n6, S)
+
+        xsg = sb("xsg", [P, S], U8)
+        nc.vector.tensor_copy(out=xsg[:], in_=xs[:].indirect(l_offs[:]))
+        wwd = sb("wwd", [P, S], U32)
+        nc.vector.tensor_copy(
+            out=wwd[:].rearrange("p (t m) -> p m t", t=PACK), in_=ww[:].rearrange("p (m t) -> p m t", t=PACK)
+        )
+        wsd = sb("wsd", [P, S], U8)
+        nc.gpsimd.tensor_copy(
+            out=wsd[:].rearrange("p (t m) -> p t m", t=PACK), in_=ws[:].rearrange("p (m t) -> p t m", t=PACK)
+        )
+        xwg = sb("xwg", [P, S], U32)
+        nc.vector.tensor_copy(out=xwg[:], in_=xw[:].indirect(l_offs[:]))
+
+        ex = sb("ex", [P, PACK, S], F32)
+        ys = []
+        for t in range(PACK):
+            cols = slice(P * t, P * (t + 1))
+            y_ps = psum.tile([P, S], F32, name="y_ps%d" % t, tag="bank%d" % t)
+            nc.tensor.matmul_mx(
+                out=y_ps[:],
+                lhsT=wwd[:, cols].bitcast(FP8X4),
+                lhsT_scale=wsd[:, cols],
+                rhs=xwg[:].bitcast(FP8X4),
+                rhs_scale=xsg[:],
+                start=True,
+                stop=True,
+            )
+            nc.scalar.activation(out=ex[:, t, :], in_=y_ps[:], func=ACT.Exp, scale=0.5)
+            y_t = sb("y%d" % t, [P, S], F32)
+            nc.vector.tensor_copy(out=y_t[:], in_=y_ps[:])
+            ys.append(y_t)
+
+        zb = sb("zb", [P, PACK, S], BF16)
+        pbs = []
+        for t in range(PACK):
+            pb = sb("pb%d" % t, [P, W], F32)
+            nc.scalar.activation(out=pb[:], in_=ys[t][:].indirect(l_n2[:]), func=ACT.Copy)
+            pbs.append(pb)
+
+        def z_plane(t):
+            pa = sb("pa%d" % t, [P, W], F32)
+            nc.vector.tensor_copy(out=pa[:], in_=ys[t][:].indirect(l_n1[:]))
+            nc.vector.tensor_tensor(out=pa[:], in0=pa[:], in1=pbs[t][:], op=ALU.max)
+            nc.vector.tensor_copy(out=ys[t][:].indirect(l_n1[:]), in_=pa[:])
+            nc.vector.tensor_scalar(
+                out=zb[:, t, :], in0=ys[t][:], scalar1=ga_t[:, t : t + 1], scalar2=None, op0=ALU.mult
+            )
+
+        zw = sb("zw", [P, S], U32)
+        zs = sb("zs", [P, S], U8)
+
+        def z_quantize():
+            zi = sb("zi", [P, PACK * S], BF16)
+            nc.vector.tensor_copy(
+                out=zi[:].rearrange("p (q m t) -> p m t q", q=PACK, t=PACK),
+                in_=zb[:].rearrange("p t (m q) -> p m t q", q=PACK),
+            )
+            nc.vector.quantize_mx(out=zw[:].bitcast(FP8X4), scales=zs[:], in_=zi[:])
+
+        s_ps = [psum.tile([P, S], F32, name="s_ps%d" % q) for q in range(PACK)]
+        s_last = [psum.tile([P, S], F32, name="s_last%d" % q, tag="bank%d" % q) for q in range(PACK)]
+        s_sb = [sb("s%d" % q, [P, S], F32) for q in range(PACK)]
+        s_sq = sb("s_sq", [P, PACK, S], F32)
+
+        def gather_piece(i, planes):
+            c0, c1 = Z2_PIECES[i]
+            width = c1 - c0
+            got = [sb("g%d_%d" % (k, i), [P, PACK, width], F32) for k in (3, 4, 5)]
+            nd = sb("nd%d" % i, [P, 2, PACK, width], F32)
+            for t0 in range(0, PACK, planes):
+                ts = slice(t0, t0 + planes)
+                for t in range(t0, t0 + planes):
+                    for tile, lst in zip(got, (l_n3, l_n4, l_n5)):
+                        nc.scalar.activation(
+                            out=tile[:, t, :], in_=ex[:, t, :].indirect(lst[:, c0 // 16 : c1 // 16]), func=ACT.Copy
+                        )
+                nc.vector.tensor_tensor(out=nd[:, 0, ts, :], in0=got[0][:, ts, :], in1=ex[:, ts, c0:c1], op=ALU.add)
+                nc.vector.tensor_tensor(out=nd[:, 1, ts, :], in0=got[1][:, ts, :], in1=got[2][:, ts, :], op=ALU.add)
+            return nd
+
+        def log_piece(nd):
+            nc.scalar.activation(out=nd[:], in_=nd[:], func=ACT.Ln)
+
+        def finish_piece(i, nd, banks):
+            c0, c1 = Z2_PIECES[i]
+            width = c1 - c0
+            nc.vector.tensor_tensor(out=nd[:, 0, :, :], in0=nd[:, 0, :, :], in1=nd[:, 1, :, :], op=ALU.subtract)
+            z2i = sb("z2i%d" % i, [P, PACK * width], BF16)
+            nc.vector.tensor_tensor(
+                out=z2i[:].rearrange("p (c i t) -> p c t i", i=4, t=PACK),
+                in0=nd[:, 0, :, :].rearrange("p t (c i) -> p c t i", i=4),
+                in1=gb_t[:].unsqueeze(1).unsqueeze(3).to_broadcast([P, width // 4, PACK, 4]),
+                op=ALU.mult,
+            )
+            z2w = sb("z2w%d" % i, [P, width], U32)
+            z2s = sb("z2s%d" % i, [P, width], U8)
+            nc.vector.quantize_mx(out=z2w[:].bitcast(FP8X4), scales=z2s[:], in_=z2i[:])
+            for q in range(PACK):
+                cols = slice(P * q, P * (q + 1))
+                nc.tensor.matmul_mx(
+                    out=banks[q][:, c0:c1],
+                    lhsT=zw[:, cols].bitcast(FP8X4),
+                    lhsT_scale=zs[:, cols],
+                    rhs=z2w[:].bitcast(FP8X4),
+                    rhs_scale=z2s[:],
+                    start=True,
+                    stop=True,
+                )
+
+        def take_out(c0, c1, banks):
+            for q in range(PACK):
+                nc.vector.tensor_scalar(
+                    out=s_sb[q][:, c0:c1], in0=banks[q][:, c0:c1], scalar1=0.0625, scalar2=None, op0=ALU.mult
+                )
+
+        def square_s(c0, c1, on_vector):
+            for q in range(PACK):
+                if on_vector:
+                    nc.vector.tensor_tensor(
+                        out=s_sq[:, q, c0:c1], in0=s_sb[q][:, c0:c1], in1=s_sb[q][:, c0:c1], op=ALU.mult
+                    )
+                else:
+                    nc.scalar.activation(out=s_sq[:, q, c0:c1], in_=s_sb[q][:, c0:c1], func=ACT.Square)
+
+        z_plane(0)
+        z_plane(1)
+        z_plane(2)
+        nd0 = gather_piece(0, 4)
+        z_plane(3)
+        nd1 = gather_piece(1, 4)
+        log_piece(nd0)
+        log_piece(nd1)
+        z_quantize()
+        finish_piece(0, nd0, s_ps)
+        finish_piece(1, nd1, s_ps)
+        ndL = gather_piece(2, 1)
+        log_piece(ndL)
+        finish_piece(2, ndL, s_last)
+        take_out(384, 512, s_last)
+        take_out(0, 384, s_ps)
+        square_s(0, 384, False)
+
+        out_rows = out_0.rearrange("(p t) j -> p t j", t=PACK)
+        out_words = out_1[0].rearrange("p n t -> p (n t)").bitcast(I32)
+        ow = sb("ow", [P, S], U32)
+        osc = sb("osc", [P, S], U8)
+        unit = 0
+        for h, (c0, c1) in enumerate(OUT_PIECES):
+            width = c1 - c0
+            res = sb("res%d" % h, [P, PACK, width], F32)
+            if h == 1:
+                square_s(384, 512, False)
+            for q in range(PACK):
+                b = sb("b%d_%d" % (h, q), [P, width], F32)
+                nc.scalar.activation(
+                    out=b[:], in_=s_sb[q][:].indirect(l_n6[:, c0 // 16 : c1 // 16]), func=ACT.Copy
+                )
+                den = sb("den%d_%d" % (h, q), [P, width], F32)
+                if unit < 2:
+                    nc.vector.tensor_tensor(out=den[:], in0=b[:], in1=b[:], op=ALU.mult)
+                else:
+                    nc.scalar.activation(out=den[:], in_=b[:], func=ACT.Square)
+                nc.vector.scalar_tensor_tensor(
+                    out=den[:], in0=den[:], scalar=0.5, in1=s_sq[:, q, c0:c1], op0=ALU.add, op1=ALU.add
+                )
+                nc.vector.tensor_tensor(out=b[:], in0=b[:], in1=s_sb[q][:, c0:c1], op=ALU.mult)
+                nc.scalar.activation(out=den[:], in_=den[:], func=ACT.Abs_reciprocal_sqrt, scale=0.5)
+                if unit >= 4:
+                    nc.scalar.activation(out=den[:], in_=den[:], func=ACT.Square)
+                else:
+                    nc.vector.tensor_tensor(out=b[:], in0=b[:], in1=den[:], op=ALU.mult)
+                nc.vector.tensor_tensor(out=res[:, q, :], in0=b[:], in1=den[:], op=ALU.mult)
+                nc.sync.dma_start(out=out_rows[:, q, c0:c1], in_=res[:, q, :])
+                unit = unit + 1
+            oi = sb("oi%d" % h, [P, PACK * width], BF16)
+            nc.vector.tensor_copy(
+                out=oi[:].rearrange("p (c i t) -> p c t i", i=4, t=PACK),
+                in_=res[:].rearrange("p t (c i) -> p c t i", i=4),
+            )
+            nc.vector.quantize_mx(out=ow[:, c0:c1].bitcast(FP8X4), scales=osc[:, c0:c1], in_=oi[:])
+            nc.sync.dma_start(out=out_words[:, c0:c1], in_=ow[:, c0:c1].bitcast(I32))
+        for q in range(4):
+            queue = nc.scalar if q < 3 else nc.sync
+            queue.dma_start(out=out_2[0, 4 * q : 4 * q + 4, :].bitcast(I32), in_=scale_rows(osc, q))

@@ -17,7 +17,7 @@ PACK = 4
 T, S, W = 2048, 512, 256
 FLOPS = 2 * 2 * 512 * 512 * 512
 
-Z2_PIECES = ((0, 256), (256, 384), (384, 512))
+Z2_PIECES = ((0, 384), (384, 512))
 OUT_PIECES = ((0, 256), (256, 512))
 
 
@@ -56,9 +56,9 @@ def tile_picked_selffilloddsharm_none_po_kernel(
         load_scales(nc.scalar, ws, w1_scales, 0)
         nc.sync.dma_start(out=xw[:].bitcast(I32), in_=x_words[0].rearrange("p n t -> p (n t)").bitcast(I32))
         load_scales(nc.scalar, ws, w1_scales, 1)
-        nc.sync.dma_start(out=ww[:].bitcast(I32), in_=w1_words[0].rearrange("p n t -> p (n t)").bitcast(I32))
-        load_scales(nc.scalar, ws, w1_scales, 2)
+        load_scales(nc.sync, ws, w1_scales, 2)
         load_scales(nc.scalar, ws, w1_scales, 3)
+        nc.sync.dma_start(out=ww[:].bitcast(I32), in_=w1_words[0].rearrange("p n t -> p (n t)").bitcast(I32))
         l_n2 = load_list("l_n2", n2, W)
         l_n1 = load_list("l_n1", n1, W)
         ga_t = sb("ga_t", [P, PACK], F32)
@@ -72,19 +72,18 @@ def tile_picked_selffilloddsharm_none_po_kernel(
 
         xsg = sb("xsg", [P, S], U8)
         nc.vector.tensor_copy(out=xsg[:], in_=xs[:].indirect(l_offs[:]))
-        wwd = sb("wwd", [P, S], U32)
-        nc.vector.tensor_copy(
-            out=wwd[:].rearrange("p (t m) -> p m t", t=PACK), in_=ww[:].rearrange("p (m t) -> p m t", t=PACK)
-        )
         wsd = sb("wsd", [P, S], U8)
         nc.gpsimd.tensor_copy(
             out=wsd[:].rearrange("p (t m) -> p t m", t=PACK), in_=ws[:].rearrange("p (m t) -> p t m", t=PACK)
         )
         xwg = sb("xwg", [P, S], U32)
         nc.vector.tensor_copy(out=xwg[:], in_=xw[:].indirect(l_offs[:]))
+        wwd = sb("wwd", [P, S], U32)
+        nc.scalar.copy(
+            out=wwd[:].rearrange("p (t m) -> p m t", t=PACK), in_=ww[:].rearrange("p (m t) -> p m t", t=PACK)
+        )
 
-        ex = sb("ex", [P, PACK, S], F32)
-        ys = []
+        exs, ys = [], []
         for t in range(PACK):
             cols = slice(P * t, P * (t + 1))
             y_ps = psum.tile([P, S], F32, name="y_ps%d" % t, tag="bank%d" % t)
@@ -97,10 +96,18 @@ def tile_picked_selffilloddsharm_none_po_kernel(
                 start=True,
                 stop=True,
             )
-            nc.scalar.activation(out=ex[:, t, :], in_=y_ps[:], func=ACT.Exp, scale=0.5)
+            ex_t = sb("ex%d" % t, [P, S], F32)
+            nc.scalar.activation(out=ex_t[:], in_=y_ps[:], func=ACT.Exp, scale=0.5)
+            exs.append(ex_t)
             y_t = sb("y%d" % t, [P, S], F32)
             nc.vector.tensor_copy(out=y_t[:], in_=y_ps[:])
             ys.append(y_t)
+
+        def interleave(dst, src):
+            nc.vector.tensor_copy(
+                out=dst.rearrange("p (c i t) -> p c t i", i=4, t=PACK),
+                in_=src.rearrange("p t (c i) -> p c t i", i=4),
+            )
 
         zb = sb("zb", [P, PACK, S], BF16)
         pbs = []
@@ -115,7 +122,11 @@ def tile_picked_selffilloddsharm_none_po_kernel(
             nc.vector.tensor_tensor(out=pa[:], in0=pa[:], in1=pbs[t][:], op=ALU.max)
             nc.vector.tensor_copy(out=ys[t][:].indirect(l_n1[:]), in_=pa[:])
             nc.vector.tensor_scalar(
-                out=zb[:, t, :], in0=ys[t][:], scalar1=ga_t[:, t : t + 1], scalar2=None, op0=ALU.mult
+                out=zb[:, t, :].rearrange("p (q m) -> p m q", q=PACK),
+                in0=ys[t][:].rearrange("p (m q) -> p m q", q=PACK),
+                scalar1=ga_t[:, t : t + 1],
+                scalar2=None,
+                op0=ALU.mult,
             )
 
         zw = sb("zw", [P, S], U32)
@@ -123,61 +134,67 @@ def tile_picked_selffilloddsharm_none_po_kernel(
 
         def z_quantize():
             zi = sb("zi", [P, PACK * S], BF16)
-            nc.vector.tensor_copy(
-                out=zi[:].rearrange("p (q m t) -> p m t q", q=PACK, t=PACK),
-                in_=zb[:].rearrange("p t (m q) -> p m t q", q=PACK),
-            )
+            interleave(zi[:], zb[:])
             nc.vector.quantize_mx(out=zw[:].bitcast(FP8X4), scales=zs[:], in_=zi[:])
 
         s_ps = [psum.tile([P, S], F32, name="s_ps%d" % q) for q in range(PACK)]
         s_last = [psum.tile([P, S], F32, name="s_last%d" % q, tag="bank%d" % q) for q in range(PACK)]
         s_sb = [sb("s%d" % q, [P, S], F32) for q in range(PACK)]
         s_sq = sb("s_sq", [P, PACK, S], F32)
+        sums, logs, z2b = {}, {}, {}
 
-        def gather_piece(i, planes):
+        def open_piece(i, got_tag, sums_tag):
+            width = Z2_PIECES[i][1] - Z2_PIECES[i][0]
+            got = pool.tile([P, PACK, 3, width], F32, name="got%d" % i, tag=got_tag, align_bytes=64)
+            sums[i] = pool.tile([P, PACK, 2, width], F32, name="sums%d" % i, tag=sums_tag, align_bytes=64)
+            logs[i] = sb("logs%d" % i, [P, PACK, 2, width], F32)
+            z2b[i] = sb("z2b%d" % i, [P, PACK, width], BF16)
+            return got
+
+        def gather_plane(i, got, t):
             c0, c1 = Z2_PIECES[i]
-            width = c1 - c0
-            got = [sb("g%d_%d" % (k, i), [P, PACK, width], F32) for k in (3, 4, 5)]
-            nd = sb("nd%d" % i, [P, 2, PACK, width], F32)
-            for t0 in range(0, PACK, planes):
-                ts = slice(t0, t0 + planes)
-                for t in range(t0, t0 + planes):
-                    for tile, lst in zip(got, (l_n3, l_n4, l_n5)):
-                        nc.scalar.activation(
-                            out=tile[:, t, :], in_=ex[:, t, :].indirect(lst[:, c0 // 16 : c1 // 16]), func=ACT.Copy
-                        )
-                nc.vector.tensor_tensor(out=nd[:, 0, ts, :], in0=got[0][:, ts, :], in1=ex[:, ts, c0:c1], op=ALU.add)
-                nc.vector.tensor_tensor(out=nd[:, 1, ts, :], in0=got[1][:, ts, :], in1=got[2][:, ts, :], op=ALU.add)
-            return nd
+            for k, lst in enumerate((l_n3, l_n4, l_n5)):
+                nc.scalar.activation(
+                    out=got[:, t, k, :], in_=exs[t][:].indirect(lst[:, c0 // 16 : c1 // 16]), func=ACT.Copy
+                )
+            nc.vector.tensor_tensor(out=sums[i][:, t, 0, :], in0=got[:, t, 0, :], in1=exs[t][:, c0:c1], op=ALU.add)
+            nc.vector.tensor_tensor(out=sums[i][:, t, 1, :], in0=got[:, t, 1, :], in1=got[:, t, 2, :], op=ALU.add)
 
-        def log_piece(nd):
-            nc.scalar.activation(out=nd[:], in_=nd[:], func=ACT.Ln)
+        def log_planes(i, t0, t1):
+            lg = logs[i]
+            nc.scalar.activation(out=lg[:, t0:t1, :, :], in_=sums[i][:, t0:t1, :, :], func=ACT.Ln)
 
-        def finish_piece(i, nd, banks):
-            c0, c1 = Z2_PIECES[i]
-            width = c1 - c0
-            nc.vector.tensor_tensor(out=nd[:, 0, :, :], in0=nd[:, 0, :, :], in1=nd[:, 1, :, :], op=ALU.subtract)
-            z2i = sb("z2i%d" % i, [P, PACK * width], BF16)
+        def scale_planes(i, t0, t1):
+            lg = logs[i]
             nc.vector.tensor_tensor(
-                out=z2i[:].rearrange("p (c i t) -> p c t i", i=4, t=PACK),
-                in0=nd[:, 0, :, :].rearrange("p t (c i) -> p c t i", i=4),
-                in1=gb_t[:].unsqueeze(1).unsqueeze(3).to_broadcast([P, width // 4, PACK, 4]),
-                op=ALU.mult,
+                out=lg[:, t0:t1, 0, :], in0=lg[:, t0:t1, 0, :], in1=lg[:, t0:t1, 1, :], op=ALU.subtract
             )
+            for t in range(t0, t1):
+                nc.vector.tensor_scalar(
+                    out=z2b[i][:, t, :], in0=lg[:, t, 0, :], scalar1=gb_t[:, t : t + 1], scalar2=None, op0=ALU.mult
+                )
+
+        def finish_piece(i, banks):
+            c0, c1 = Z2_PIECES[i]
+            width = c1 - c0
+            z2i = sb("z2i%d" % i, [P, PACK * width], BF16)
+            interleave(z2i[:], z2b[i][:])
             z2w = sb("z2w%d" % i, [P, width], U32)
             z2s = sb("z2s%d" % i, [P, width], U8)
             nc.vector.quantize_mx(out=z2w[:].bitcast(FP8X4), scales=z2s[:], in_=z2i[:])
             for q in range(PACK):
                 cols = slice(P * q, P * (q + 1))
-                nc.tensor.matmul_mx(
-                    out=banks[q][:, c0:c1],
-                    lhsT=zw[:, cols].bitcast(FP8X4),
-                    lhsT_scale=zs[:, cols],
-                    rhs=z2w[:].bitcast(FP8X4),
-                    rhs_scale=z2s[:],
-                    start=True,
-                    stop=True,
-                )
+                for n0 in range(0, width, 256):
+                    n1_ = min(n0 + 256, width)
+                    nc.tensor.matmul_mx(
+                        out=banks[q][:, c0 + n0 : c0 + n1_],
+                        lhsT=zw[:, cols].bitcast(FP8X4),
+                        lhsT_scale=zs[:, cols],
+                        rhs=z2w[:, n0:n1_].bitcast(FP8X4),
+                        rhs_scale=z2s[:, n0:n1_],
+                        start=True,
+                        stop=True,
+                    )
 
         def take_out(c0, c1, banks):
             for q in range(PACK):
@@ -185,32 +202,36 @@ def tile_picked_selffilloddsharm_none_po_kernel(
                     out=s_sb[q][:, c0:c1], in0=banks[q][:, c0:c1], scalar1=0.0625, scalar2=None, op0=ALU.mult
                 )
 
-        def square_s(c0, c1, on_vector):
+        def square_s(c0, c1):
             for q in range(PACK):
-                if on_vector:
-                    nc.vector.tensor_tensor(
-                        out=s_sq[:, q, c0:c1], in0=s_sb[q][:, c0:c1], in1=s_sb[q][:, c0:c1], op=ALU.mult
-                    )
-                else:
-                    nc.scalar.activation(out=s_sq[:, q, c0:c1], in_=s_sb[q][:, c0:c1], func=ACT.Square)
+                nc.scalar.activation(out=s_sq[:, q, c0:c1], in_=s_sb[q][:, c0:c1], func=ACT.Square)
 
         z_plane(0)
         z_plane(1)
+        got = open_piece(0, "got0", "sums0")
+        gather_plane(0, got, 0)
         z_plane(2)
-        nd0 = gather_piece(0, 4)
+        gather_plane(0, got, 1)
         z_plane(3)
-        nd1 = gather_piece(1, 4)
-        log_piece(nd0)
-        log_piece(nd1)
+        gather_plane(0, got, 2)
+        gather_plane(0, got, 3)
         z_quantize()
-        finish_piece(0, nd0, s_ps)
-        finish_piece(1, nd1, s_ps)
-        ndL = gather_piece(2, 1)
-        log_piece(ndL)
-        finish_piece(2, ndL, s_last)
+        for t in range(PACK):
+            log_planes(0, t, t + 1)
+        got = open_piece(1, "sums0", "sums1")
+        scale_planes(0, 0, 2)
+        scale_planes(0, 2, 4)
+        finish_piece(0, s_ps)
+        for t in range(PACK):
+            gather_plane(1, got, t)
+        log_planes(1, 0, 3)
+        log_planes(1, 3, 4)
+        scale_planes(1, 0, 3)
+        scale_planes(1, 3, 4)
+        finish_piece(1, s_last)
         take_out(384, 512, s_last)
         take_out(0, 384, s_ps)
-        square_s(0, 384, False)
+        square_s(0, 384)
 
         out_rows = out_0.rearrange("(p t) j -> p t j", t=PACK)
         out_words = out_1[0].rearrange("p n t -> p (n t)").bitcast(I32)
@@ -221,14 +242,18 @@ def tile_picked_selffilloddsharm_none_po_kernel(
             width = c1 - c0
             res = sb("res%d" % h, [P, PACK, width], F32)
             if h == 1:
-                square_s(384, 512, False)
+                square_s(384, 512)
             for q in range(PACK):
                 b = sb("b%d_%d" % (h, q), [P, width], F32)
-                nc.scalar.activation(
-                    out=b[:], in_=s_sb[q][:].indirect(l_n6[:, c0 // 16 : c1 // 16]), func=ACT.Copy
-                )
+                for g0 in range(c0, c1, 256):
+                    g1 = min(g0 + 256, c1)
+                    nc.scalar.activation(
+                        out=b[:, g0 - c0 : g1 - c0],
+                        in_=s_sb[q][:].indirect(l_n6[:, g0 // 16 : g1 // 16]),
+                        func=ACT.Copy,
+                    )
                 den = sb("den%d_%d" % (h, q), [P, width], F32)
-                if unit < 2:
+                if unit < 1:
                     nc.vector.tensor_tensor(out=den[:], in0=b[:], in1=b[:], op=ALU.mult)
                 else:
                     nc.scalar.activation(out=den[:], in_=b[:], func=ACT.Square)
@@ -237,7 +262,7 @@ def tile_picked_selffilloddsharm_none_po_kernel(
                 )
                 nc.vector.tensor_tensor(out=b[:], in0=b[:], in1=s_sb[q][:, c0:c1], op=ALU.mult)
                 nc.scalar.activation(out=den[:], in_=den[:], func=ACT.Abs_reciprocal_sqrt, scale=0.5)
-                if unit >= 4:
+                if unit % 2 == 1:
                     nc.scalar.activation(out=den[:], in_=den[:], func=ACT.Square)
                 else:
                     nc.vector.tensor_tensor(out=b[:], in0=b[:], in1=den[:], op=ALU.mult)

@@ -231,6 +231,8 @@ def tile_picked_selffilloddsharm_none_po_kernel(
         finish_piece(1, s_last)
         take_out(384, 512, s_last)
         take_out(0, 384, s_ps)
+        warm = sb("warm", [P, 1], F32)
+        nc.scalar.activation(out=warm[:], in_=logs[len(Z2_PIECES) - 1][:, 3, 1, 0:1], func=ACT.Abs_reciprocal_sqrt)
         square_s(0, 384)
 
         out_rows = out_0.rearrange("(p t) j -> p t j", t=PACK)

from contextlib import ExitStack

import concourse.mybir as mybir

F32 = mybir.dt.float32
BF16 = mybir.dt.bfloat16
I32 = mybir.dt.int32
U32 = mybir.dt.uint32
U16 = mybir.dt.uint16
U8 = mybir.dt.uint8
FP8X4 = mybir.dt.float8_e4m3fn_x4
ACT = mybir.ActivationFunctionType
ALU = mybir.AluOpType

P = 128
PACK = 4
T, S, W = 2048, 512, 256
FLOPS = 2 * 2 * 512 * 512 * 512

Z2_PIECES = ((0, 384), (384, 512))
OUT_PIECES = ((0, 256), (256, 512))


def tile_picked_selffilloddsharm_none_po_kernel(
    tc, x_words, x_scales, w1_words, w1_scales, ga, gb, offs, n1, n2, n3, n4, n5, n6, out_0, out_1, out_2
):
    nc = tc.nc
    with ExitStack() as ctx:
        pool = ctx.enter_context(tc.tile_pool(name="held", bufs=1))
        psum = ctx.enter_context(tc.psum_pool(name="psum", bufs=1))

        def sb(name, shape, dtype):
            return pool.tile(shape, dtype, name=name, align_bytes=64)

        def load_list(name, src, entries):
            tile = sb(name, [P, entries // 16], U16)
            nc.sync.dma_start(tile[:], src)
            return tile

        def scale_rows(tile, q):
            return tile[32 * q : 32 * q + 4, :].bitcast(I32)

        def load_scales(queue, tile, src, q):
            rows = src[0, 4 * q : 4 * q + 4, :].bitcast(I32)
            queue.dma_start(out=tile[32 * q : 32 * q + 32, :].bitcast(I32), in_=rows.partition_broadcast(8))

        xs = sb("xs", [P, T], U8)
        ws = sb("ws", [P, S], U8)
        xw = sb("xw", [P, T], U32)
        ww = sb("ww", [P, S], U32)
        l_offs = load_list("l_offs", offs, S)
        load_scales(nc.scalar, xs, x_scales, 2)
        load_scales(nc.sync, xs, x_scales, 0)
        load_scales(nc.scalar, xs, x_scales, 3)
        load_scales(nc.sync, xs, x_scales, 1)
        load_scales(nc.scalar, ws, w1_scales, 0)
        nc.sync.dma_start(out=xw[:].bitcast(I32), in_=x_words[0].rearrange("p n t -> p (n t)").bitcast(I32))
        load_scales(nc.scalar, ws, w1_scales, 1)
        load_scales(nc.sync, ws, w1_scales, 2)
        load_scales(nc.scalar, ws, w1_scales, 3)
        nc.sync.dma_start(out=ww[:].bitcast(I32), in_=w1_words[0].rearrange("p n t -> p (n t)").bitcast(I32))
        l_n2 = load_list("l_n2", n2, W)
        l_n1 = load_list("l_n1", n1, W)
        ga_t = sb("ga_t", [P, PACK], F32)
        nc.sync.dma_start(out=ga_t[:], in_=ga.rearrange("(p t) o -> p (t o)", t=PACK))
        l_n3 = load_list("l_n3", n3, S)
        l_n4 = load_list("l_n4", n4, S)
        l_n5 = load_list("l_n5", n5, S)
        gb_t = sb("gb_t", [P, PACK], F32)
        nc.sync.dma_start(out=gb_t[:], in_=gb.rearrange("(p t) o -> p (t o)", t=PACK))
        l_n6 = load_list("l_n6", n6, S)

        xsg = sb("xsg", [P, S], U8)
        nc.vector.tensor_copy(out=xsg[:], in_=xs[:].indirect(l_offs[:]))
        wsd = sb("wsd", [P, S], U8)
        nc.gpsimd.tensor_copy(
            out=wsd[:].rearrange("p (t m) -> p t m", t=PACK), in_=ws[:].rearrange("p (m t) -> p t m", t=PACK)
        )
        xwg = sb("xwg", [P, S], U32)
        nc.vector.tensor_copy(out=xwg[:], in_=xw[:].indirect(l_offs[:]))
        wwd = sb("wwd", [P, S], U32)
        nc.scalar.copy(
            out=wwd[:].rearrange("p (t m) -> p m t", t=PACK), in_=ww[:].rearrange("p (m t) -> p m t", t=PACK)
        )

        exs, ys = [], []
        for t in range(PACK):
            cols = slice(P * t, P * (t + 1))
            y_ps = psum.tile([P, S], F32, name="y_ps%d" % t, tag="bank%d" % t)
            nc.tensor.matmul_mx(
                out=y_ps[:],
                lhsT=wwd[:, cols].bitcast(FP8X4),
                lhsT_scale=wsd[:, cols],
                rhs=xwg[:].bitcast(FP8X4),
                rhs_scale=xsg[:],
                start=True,
                stop=True,
            )
            ex_t = sb("ex%d" % t, [P, S], F32)
            nc.scalar.activation(out=ex_t[:], in_=y_ps[:], func=ACT.Exp, scale=0.5)
            exs.append(ex_t)
            y_t = sb("y%d" % t, [P, S], F32)
            nc.vector.tensor_copy(out=y_t[:], in_=y_ps[:])
            ys.append(y_t)

        def interleave(dst, src):
            nc.vector.tensor_copy(
                out=dst.rearrange("p (c i t) -> p c t i", i=4, t=PACK),
                in_=src.rearrange("p t (c i) -> p c t i", i=4),
            )

        zb = sb("zb", [P, PACK, S], BF16)
        pbs = []
        for t in range(PACK):
            pb = sb("pb%d" % t, [P, W], F32)
            nc.scalar.activation(out=pb[:], in_=ys[t][:].indirect(l_n2[:]), func=ACT.Copy)
            pbs.append(pb)

        def z_plane(t):
            pa = sb("pa%d" % t, [P, W], F32)
            nc.vector.tensor_copy(out=pa[:], in_=ys[t][:].indirect(l_n1[:]))
            nc.vector.tensor_tensor(out=pa[:], in0=pa[:], in1=pbs[t][:], op=ALU.max)
            nc.vector.tensor_copy(out=ys[t][:].indirect(l_n1[:]), in_=pa[:])
            nc.vector.tensor_scalar(
                out=zb[:, t, :].rearrange("p (q m) -> p m q", q=PACK),
                in0=ys[t][:].rearrange("p (m q) -> p m q", q=PACK),
                scalar1=ga_t[:, t : t + 1],
                scalar2=None,
                op0=ALU.mult,
            )

        zw = sb("zw", [P, S], U32)
        zs = sb("zs", [P, S], U8)

        def z_quantize():
            zi = sb("zi", [P, PACK * S], BF16)
            interleave(zi[:], zb[:])
            nc.vector.quantize_mx(out=zw[:].bitcast(FP8X4), scales=zs[:], in_=zi[:])

        s_ps = [psum.tile([P, S], F32, name="s_ps%d" % q) for q in range(PACK)]
        s_last = [psum.tile([P, S], F32, name="s_last%d" % q, tag="bank%d" % q) for q in range(PACK)]
        s_sb = [sb("s%d" % q, [P, S], F32) for q in range(PACK)]
        s_sq = sb("s_sq", [P, PACK, S], F32)
        sums, logs, z2b = {}, {}, {}

        def open_piece(i, got_tag, sums_tag):
            width = Z2_PIECES[i][1] - Z2_PIECES[i][0]
            got = pool.tile([P, PACK, 3, width], F32, name="got%d" % i, tag=got_tag, align_bytes=64)
            sums[i] = pool.tile([P, PACK, 2, width], F32, name="sums%d" % i, tag=sums_tag, align_bytes=64)
            logs[i] = sb("logs%d" % i, [P, PACK, 2, width], F32)
            z2b[i] = sb("z2b%d" % i, [P, PACK, width], BF16)
            return got

        def gather_plane(i, got, t):
            c0, c1 = Z2_PIECES[i]
            for k, lst in enumerate((l_n3, l_n4, l_n5)):
                nc.scalar.activation(
                    out=got[:, t, k, :], in_=exs[t][:].indirect(lst[:, c0 // 16 : c1 // 16]), func=ACT.Copy
                )
            nc.vector.tensor_tensor(out=sums[i][:, t, 0, :], in0=got[:, t, 0, :], in1=exs[t][:, c0:c1], op=ALU.add)
            nc.vector.tensor_tensor(out=sums[i][:, t, 1, :], in0=got[:, t, 1, :], in1=got[:, t, 2, :], op=ALU.add)

        def log_planes(i, t0, t1):
            lg = logs[i]
            nc.scalar.activation(out=lg[:, t0:t1, :, :], in_=sums[i][:, t0:t1, :, :], func=ACT.Ln)

        def scale_planes(i, t0, t1):
            lg = logs[i]
            nc.vector.tensor_tensor(
                out=lg[:, t0:t1, 0, :], in0=lg[:, t0:t1, 0, :], in1=lg[:, t0:t1, 1, :], op=ALU.subtract
            )
            for t in range(t0, t1):
                nc.vector.tensor_scalar(
                    out=z2b[i][:, t, :], in0=lg[:, t, 0, :], scalar1=gb_t[:, t : t + 1], scalar2=None, op0=ALU.mult
                )

        def finish_piece(i, banks):
            c0, c1 = Z2_PIECES[i]
            width = c1 - c0
            z2i = sb("z2i%d" % i, [P, PACK * width], BF16)
            interleave(z2i[:], z2b[i][:])
            z2w = sb("z2w%d" % i, [P, width], U32)
            z2s = sb("z2s%d" % i, [P, width], U8)
            nc.vector.quantize_mx(out=z2w[:].bitcast(FP8X4), scales=z2s[:], in_=z2i[:])
            for q in range(PACK):
                cols = slice(P * q, P * (q + 1))
                for n0 in range(0, width, 256):
                    n1_ = min(n0 + 256, width)
                    nc.tensor.matmul_mx(
                        out=banks[q][:, c0 + n0 : c0 + n1_],
                        lhsT=zw[:, cols].bitcast(FP8X4),
                        lhsT_scale=zs[:, cols],
                        rhs=z2w[:, n0:n1_].bitcast(FP8X4),
                        rhs_scale=z2s[:, n0:n1_],
                        start=True,
                        stop=True,
                    )

        def take_out(c0, c1, banks):
            for q in range(PACK):
                nc.vector.tensor_scalar(
                    out=s_sb[q][:, c0:c1], in0=banks[q][:, c0:c1], scalar1=0.0625, scalar2=None, op0=ALU.mult
                )

        def square_s(c0, c1):
            for q in range(PACK):
                nc.scalar.activation(out=s_sq[:, q, c0:c1], in_=s_sb[q][:, c0:c1], func=ACT.Square)

        z_plane(0)
        z_plane(1)
        got = open_piece(0, "got0", "sums0")
        gather_plane(0, got, 0)
        z_plane(2)
        gather_plane(0, got, 1)
        z_plane(3)
        gather_plane(0, got, 2)
        gather_plane(0, got, 3)
        z_quantize()
        for t in range(PACK):
            log_planes(0, t, t + 1)
        got = open_piece(1, "sums0", "sums1")
        scale_planes(0, 0, 2)
        scale_planes(0, 2, 4)
        finish_piece(0, s_ps)
        for t in range(PACK):
            gather_plane(1, got, t)
        log_planes(1, 0, 3)
        log_planes(1, 3, 4)
        scale_planes(1, 0, 3)
        scale_planes(1, 3, 4)
        finish_piece(1, s_last)
        take_out(384, 512, s_last)
        take_out(0, 384, s_ps)
        warm = sb("warm", [P, 1], F32)
        nc.scalar.activation(out=warm[:], in_=logs[len(Z2_PIECES) - 1][:, 3, 1, 0:1], func=ACT.Abs_reciprocal_sqrt)
        square_s(0, 384)

        out_rows = out_0.rearrange("(p t) j -> p t j", t=PACK)
        out_words = out_1[0].rearrange("p n t -> p (n t)").bitcast(I32)
        ow = sb("ow", [P, S], U32)
        osc = sb("osc", [P, S], U8)
        unit = 0
        for h, (c0, c1) in enumerate(OUT_PIECES):
            width = c1 - c0
            res = sb("res%d" % h, [P, PACK, width], F32)
            if h == 1:
                square_s(384, 512)
            for q in range(PACK):
                b = sb("b%d_%d" % (h, q), [P, width], F32)
                for g0 in range(c0, c1, 256):
                    g1 = min(g0 + 256, c1)
                    nc.scalar.activation(
                        out=b[:, g0 - c0 : g1 - c0],
                        in_=s_sb[q][:].indirect(l_n6[:, g0 // 16 : g1 // 16]),
                        func=ACT.Copy,
                    )
                den = sb("den%d_%d" % (h, q), [P, width], F32)
                if unit < 1:
                    nc.vector.tensor_tensor(out=den[:], in0=b[:], in1=b[:], op=ALU.mult)
                else:
                    nc.scalar.activation(out=den[:], in_=b[:], func=ACT.Square)
                nc.vector.scalar_tensor_tensor(
                    out=den[:], in0=den[:], scalar=0.5, in1=s_sq[:, q, c0:c1], op0=ALU.add, op1=ALU.add
                )
                nc.vector.tensor_tensor(out=b[:], in0=b[:], in1=s_sb[q][:, c0:c1], op=ALU.mult)
                nc.scalar.activation(out=den[:], in_=den[:], func=ACT.Abs_reciprocal_sqrt, scale=0.5)
                if unit % 2 == 1:
                    nc.scalar.activation(out=den[:], in_=den[:], func=ACT.Square)
                else:
                    nc.vector.tensor_tensor(out=b[:], in0=b[:], in1=den[:], op=ALU.mult)
                nc.vector.tensor_tensor(out=res[:, q, :], in0=b[:], in1=den[:], op=ALU.mult)
                nc.sync.dma_start(out=out_rows[:, q, c0:c1], in_=res[:, q, :])
                unit = unit + 1
            oi = sb("oi%d" % h, [P, PACK * width], BF16)
            nc.vector.tensor_copy(
                out=oi[:].rearrange("p (c i t) -> p c t i", i=4, t=PACK),
                in_=res[:].rearrange("p t (c i) -> p c t i", i=4),
            )
            nc.vector.quantize_mx(out=ow[:, c0:c1].bitcast(FP8X4), scales=osc[:, c0:c1], in_=oi[:])
            nc.sync.dma_start(out=out_words[:, c0:c1], in_=ow[:, c0:c1].bitcast(I32))
        for q in range(4):
            queue = nc.scalar if q < 3 else nc.sync
            queue.dma_start(out=out_2[0, 4 * q : 4 * q + 4, :].bitcast(I32), in_=scale_rows(osc, q))
